import numpy as np
import ml_dtypes


def mxq(x, axis, fmt="e4m3"):
    dtype, down = {"e4m3": (ml_dtypes.float8_e4m3fn, 7), "e5m2": (ml_dtypes.float8_e5m2, 14)}[fmt]
    v = np.moveaxis(np.asarray(x, np.float32).astype(ml_dtypes.bfloat16).astype(np.float64), axis, -1)
    blocks = v.reshape(v.shape[:-1] + (-1, 32))
    amax = np.abs(blocks).max(-1, keepdims=True)
    byte = np.maximum(np.where(amax > 0, np.frexp(amax)[1] - 1 + 127, 0) - down, 1)
    scale = np.exp2(byte - 127.0)
    codes = (blocks / scale).astype(np.float32).astype(dtype).astype(np.float64)
    return np.moveaxis((codes * scale).reshape(v.shape), -1, axis)


WIDE = False


def mx_kscale(k):
    if not WIDE:
        return np.ones(k)
    levels = np.array([10, -10, 5, -5, 0])
    if k % 512:
        return np.exp2(np.random.permutation(np.resize(levels, k // 32))).repeat(32)
    a = np.empty((k // 512, 16))
    for p in range(k // 512):
        a[p, :8] = np.random.permutation(np.resize(levels, 8))
        for g in range(8):
            far = levels[np.abs(levels - a[p, g]) >= 10]
            a[p, g + 8] = far[np.random.randint(len(far))]
    return np.exp2(a.ravel()).repeat(32)


BF16 = ml_dtypes.bfloat16


def bf(x):
    return np.asarray(x, np.float32).astype(BF16)


def f64(x):
    return np.asarray(x).astype(np.float64)


E2M1 = np.array([0.0, 0.5, 1.0, 1.5, 2.0, 3.0, 4.0, 6.0, -0.0, -0.5, -1.0, -1.5, -2.0, -3.0, -4.0, -6.0])


def pack_weight(w, fmt):
    k, n = w.shape
    w = f64(bf(w)).reshape(k // 32, 32, n)
    amax = np.abs(w).max(1)
    if fmt == "e4m3":
        byte = np.frexp(amax)[1] - 1 + 127 - 7
    else:
        mant, ex = np.frexp(amax / 6.0)
        byte = np.where(mant > 0.5, ex, ex - 1) + 127
    byte = np.clip(np.where(amax > 0, byte, 1), 1, 254)
    scaled = (w * np.exp2(127.0 - byte)[:, None, :]).reshape(k, n).astype(np.float32)
    by_word = np.ascontiguousarray(scaled.reshape(k // 512, 128, 4, n).transpose(0, 1, 3, 2))
    if fmt == "e4m3":
        words = by_word.astype(ml_dtypes.float8_e4m3fn).view(np.uint8)
    else:
        c = by_word.astype(ml_dtypes.float4_e2m1fn).view(np.uint8) & 0xF
        words = c[..., 0::2] | (c[..., 1::2] << 4)
    return np.ascontiguousarray(words), np.ascontiguousarray(byte.astype(np.uint8).reshape(k // 512, 16, n))


def unpack_weight(words, scales, fmt):
    g, p, n, _ = words.shape
    if fmt == "e4m3":
        vals = np.ascontiguousarray(words).view(ml_dtypes.float8_e4m3fn).astype(np.float64)
    else:
        nib = np.empty((g, p, n, 4), np.uint8)
        nib[..., 0::2] = words & 0xF
        nib[..., 1::2] = words >> 4
        vals = E2M1[nib]
    vals = vals * np.repeat(np.exp2(scales.astype(np.float64) - 127.0), 8, axis=1)[..., None]
    return vals.transpose(0, 1, 3, 2).reshape(g * 512, n)
def pack4(w):
    words, scales = pack_weight(w, "e2m1")
    return words.reshape(words.shape[0], 128, -1), scales


def unpack4(words, scales):
    return unpack_weight(words.reshape(words.shape[0], 128, -1, 2), scales, "e2m1")


def planes(Y):
    n, m = Y.shape
    b = f64(bf(Y)).reshape(n // 32, 32, m)
    amax = np.abs(b).max(1)
    byte = np.clip(np.where(amax > 0, np.frexp(amax)[1] - 1 + 127 - 7, 1), 1, 254)
    codes = (b * np.exp2(127.0 - byte)[:, None, :]).reshape(n, m).astype(np.float32).astype(ml_dtypes.float8_e4m3fn).view(np.uint8)
    words = codes.reshape(n // 512, 128, 4, m).transpose(0, 1, 3, 2)
    return np.ascontiguousarray(words), np.ascontiguousarray(byte.astype(np.uint8).reshape(n // 512, 16, m))


TOK, EXP, CAP, D = 2048, 8, 192, 1024


def setup_inputs():
    s = mx_kscale(TOK)
    size = np.exp(0.7 * np.random.randn(D))
    x = np.random.randn(TOK, D) * size[None, :]
    sel = np.exp(np.random.randn(TOK, EXP, CAP) - 1.0) / np.sqrt(TOK)
    place = np.arange(CAP) / CAP
    logit = 2.5 - 3.0 * place[None, :] + 0.7 * np.random.randn(EXP, CAP)
    default = 0.5 * np.random.randn(EXP, D) * size[None, :]
    x_words, x_scales = pack_weight(x / s[:, None], "e4m3")
    return {
        "x_words": x_words,
        "x_scales": x_scales,
        "select": bf(sel * s[:, None, None]),
        "capacity_logit": bf(logit),
        "default_vec": bf(default),
    }

def reference(x_words, x_scales, select, capacity_logit, default_vec):
    x = unpack_weight(x_words, x_scales, "e4m3")
    sel = mxq(f64(select).reshape(TOK, EXP * CAP), 0, "e4m3")
    z = (sel.T @ x).reshape(EXP, CAP, D)
    mask = 1.0 / (1.0 + np.exp(-f64(capacity_logit)))
    base = f64(default_vec)[:, None, :]
    y = base + mask[:, :, None] * (z - base)
    Y = y.reshape(EXP * CAP, D).T
    words, scales = planes(Y)
    return y, words, scales

@@ -1,0 +1,315 @@
+from contextlib import ExitStack
+
+import concourse.mybir as mybir
+from concourse.masks import make_identity
+
+TOK, EXP, CAP, D = 2048, 8, 192, 1024
+SLOTS = EXP * CAP
+FLOPS = 2 * TOK * SLOTS * D
+
+F32 = mybir.dt.float32
+BF16 = mybir.dt.bfloat16
+I32 = mybir.dt.int32
+U32 = mybir.dt.uint32
+U8 = mybir.dt.uint8
+FP8X4 = mybir.dt.float8_e4m3fn_x4
+ACT = mybir.ActivationFunctionType
+ALU = mybir.AluOpType
+
+P = 128
+PACK = 4
+PASSES = TOK // (P * PACK)
+HALF = 512
+TILES = SLOTS // P
+CHUNKS = [[0, 1, 2], [3, 4], [5, 6, 7], [8, 9, 10, 11]]
+GROUPS = [(0, 1), (2, 3), (4, 5), (6, 7), (8,), (9,), (10,), (11,)]
+
+
+def tile_soft_capacity_dispatch_g6_kernel(
+    tc, x_words, x_scales, select, capacity_logit, default_vec, out_0, out_1, out_2
+):
+    nc = tc.nc
+    sel_rows = select.rearrange("k e c -> k (e c)")
+    y_rows = out_0.rearrange("e c d -> (e c) d")
+    codes_hbm = out_1.rearrange("h p m t -> p h (m t)").bitcast(I32)
+    scales_hbm = out_2.rearrange("h q m -> q h m")
+    chunk_of = {j: c for c, js in enumerate(CHUNKS) for j in js}
+    group_of = {j: js for js in GROUPS for j in js}
+    first = CHUNKS[0]
+
+    with ExitStack() as ctx:
+        keep = ctx.enter_context(tc.tile_pool(name="keep", bufs=1))
+        ring = ctx.enter_context(tc.tile_pool(name="ring", bufs=3))
+        psum = ctx.enter_context(tc.psum_pool(name="psum", bufs=1))
+        ctx.enter_context(tc.manual_schedule())
+
+        ident = keep.tile([P, P], F32)
+        ident_bf = keep.tile([P, P], BF16)
+        warm = keep.tile([P, 8], F32)
+        warm_out = keep.tile([P, 8], F32)
+        logit_rows = keep.tile([P, P], BF16)
+        base_rows = keep.tile([P, EXP, 16], BF16)
+        mask = keep.tile([P, 16], F32)
+        rest = keep.tile([P, 16], F32)
+        x_codes = keep.tile([P, PASSES, D], U32, align_bytes=64)
+        x_plane = keep.tile([P, D], U8, align_bytes=64)
+        raw = [keep.tile([P, PASSES, PACK, P * len(js)], BF16, name="raw%d" % c) for c, js in enumerate(CHUNKS)]
+        sel_codes = keep.tile([P, TILES * PASSES * P], U32, align_bytes=64)
+        sel_plane = keep.tile([P, TILES * PASSES * P], U8, align_bytes=64)
+        y = [keep.tile([P, D], F32, name="y%d" % j) for j in range(TILES)]
+        y_codes = keep.tile([P, 2, SLOTS], U32, align_bytes=64)
+        y_plane = keep.tile([P, 2, SLOTS], U8, align_bytes=64)
+        staged, sums, base_bank, y_pairs, turned, y_turned = {}, {}, {}, {}, {}, {}
+
+        def engine(name):
+            return nc.vector if name == "V" else nc.scalar
+
+        def copy(name, out, in_):
+            if name == "V":
+                nc.vector.tensor_copy(out=out, in_=in_)
+            else:
+                nc.scalar.copy(out=out, in_=in_)
+
+        def bank(b, dtype=F32, width=HALF):
+            return psum.tile([P, width], dtype, name="bank%d" % b, tag="bank%d" % b)
+
+        def sel_cols(j, g):
+            start = (g * len(first) + j) * P if j in first else (j * PASSES + g) * P
+            return slice(start, start + P)
+
+        def load_sel(c, g):
+            js = CHUNKS[c]
+            rows = sel_rows[g * P * PACK : (g + 1) * P * PACK, js[0] * P : (js[-1] + 1) * P]
+            nc.sync.dma_start(out=raw[c][:, g], in_=rows.rearrange("(p t) w -> p t w", t=PACK))
+
+        def load_x(g):
+            nc.sync.dma_start(out=x_codes[:, g, :].bitcast(I32), in_=x_words[g].rearrange("p n t -> p (n t)").bitcast(I32))
+
+        def I0(g, name):
+            width = P * len(first)
+            staged["first", g] = ring.tile([P, PASSES * P * PACK], BF16, name="staged", tag="staged", align_bytes=64)
+            dst = staged["first", g][:, : width * PACK].rearrange("p (c i t) -> p c t i", i=4, t=PACK)
+            copy(name, dst, raw[0][:, g].rearrange("p t (c i) -> p c t i", i=4))
+
+        def Q0(g):
+            width = P * len(first)
+            for lo, hi in ((0, 256), (256, width)):
+                cols = slice(g * width + lo, g * width + hi)
+                nc.vector.quantize_mx(
+                    out=sel_codes[:, cols].bitcast(FP8X4),
+                    scales=sel_plane[:, cols],
+                    in_=staged["first", g][:, lo * PACK : hi * PACK],
+                )
+
+        def I(j, name, gs):
+            if j not in staged:
+                staged[j] = ring.tile([P, PASSES * P * PACK], BF16, name="staged", tag="staged", align_bytes=64)
+            c = chunk_of[j]
+            off = (j - CHUNKS[c][0]) * P
+            g0, g1 = gs[0], gs[-1] + 1
+            dst = staged[j][:].rearrange("p (g c i t) -> p g c t i", g=PASSES, i=4, t=PACK)[:, g0:g1]
+            src = raw[c][:, g0:g1, :, off : off + P].rearrange("p g t (c i) -> p g c t i", i=4)
+            copy(name, dst, src)
+
+        def Q(j):
+            cols = slice(j * PASSES * P, (j + 1) * PASSES * P)
+            nc.vector.quantize_mx(out=sel_codes[:, cols].bitcast(FP8X4), scales=sel_plane[:, cols], in_=staged[j][:])
+
+        def mm(j, h, g):
+            if g == 0:
+                sums[j, h] = bank(2 * j + h if j in first else 2 * ((j + 1) % 2) + h)
+            d_cols = slice(h * HALF, (h + 1) * HALF)
+            nc.tensor.matmul_mx(
+                out=sums[j, h][:],
+                lhsT=sel_codes[:, sel_cols(j, g)].bitcast(FP8X4),
+                lhsT_scale=sel_plane[:, sel_cols(j, g)],
+                rhs=x_codes[:, g, d_cols].bitcast(FP8X4),
+                rhs_scale=x_plane[4 * g : P, d_cols],
+                start=(g == 0),
+                stop=(g == PASSES - 1),
+            )
+
+        def MM0(g, j):
+            for h in range(2):
+                mm(j, h, g)
+
+        def MM(j, h):
+            for g in range(PASSES):
+                mm(j, h, g)
+
+        def BE(e, b):
+            base_bank[e] = bank(b)
+            words = base_rows[:].bitcast(F32)
+            for w in range(4):
+                nc.tensor.transpose(
+                    base_bank[e][:, w * P : (w + 1) * P], words[:, e, w : w + 1].to_broadcast([P, P]), ident[:]
+                )
+
+        def BD(j, part, name):
+            mixed = j % 3 == 1
+            e = 2 * (j // 3) + (0 if j % 3 == 0 or (mixed and part == "a") else 1)
+            rows = slice(0, P) if not mixed else (slice(0, 64) if part == "a" else slice(64, P))
+            src = base_bank[e][rows, :].bitcast(BF16).rearrange("p (w n b) -> p n w b", w=4, b=2)
+            dst = y[j][rows, :].rearrange("p (n w b) -> p n w b", w=4, b=2)
+            if name == "V":
+                nc.vector.tensor_scalar(out=dst, in0=src, scalar1=rest[rows, j : j + 1], scalar2=None, op0=ALU.mult)
+            else:
+                nc.scalar.activation(out=dst, in_=src, func=ACT.Copy, scale=rest[rows, j : j + 1])
+
+        def E(j, h):
+            part = y[j][:, h * HALF : (h + 1) * HALF]
+            nc.vector.scalar_tensor_tensor(
+                out=part, in0=sums[j, h][:], scalar=mask[:, j : j + 1], in1=part, op0=ALU.mult, op1=ALU.add
+            )
+
+        def C(j, hs, name):
+            if j not in y_pairs:
+                y_pairs[j] = ring.tile([P, D], BF16, name="y_pairs", tag="y_pairs")
+            h0, h1 = hs[0], hs[-1] + 1
+            dst = y_pairs[j][:].rearrange("p (h u q e) -> p h u q e", h=2, u=2, e=2)[:, h0:h1]
+            src = y[j][:].rearrange("p (h q u e) -> p h u q e", h=2, u=2, e=2)[:, h0:h1]
+            copy(name, dst, src)
+
+        def T(j, hs):
+            if j not in turned:
+                turned[j] = bank(6 + j % 2)
+            words = y_pairs[j][:].bitcast(F32)
+            for h in hs:
+                for u in range(2):
+                    cols = slice((2 * h + u) * P, (2 * h + u + 1) * P)
+                    nc.tensor.transpose(turned[j][:, cols], words[:, cols], ident[:])
+
+        def X(j, hs, name):
+            js = group_of[j]
+            if js not in y_turned:
+                y_turned[js] = ring.tile([P, 2, 2 * P * PACK], BF16, name="y_turned", tag="y_turned", align_bytes=64)
+            off = (j - js[0]) * P
+            h0, h1 = hs[0], hs[-1] + 1
+            dst = y_turned[js][:].bitcast(F32).rearrange("p h (r u) -> p h r u", u=2)[:, h0:h1, off : off + P, :]
+            src = turned[j][:].rearrange("p (h u r) -> p h r u", h=2, u=2)[:, h0:h1]
+            copy(name, dst, src)
+
+        def Z(js, h):
+            js = tuple(js)
+            cols = slice(js[0] * P, (js[-1] + 1) * P)
+            nc.vector.quantize_mx(
+                out=y_codes[:, h, cols].bitcast(FP8X4),
+                scales=y_plane[:, h, cols],
+                in_=y_turned[js][:, h, : len(js) * P * PACK],
+            )
+
+        def Sy(j, hs):
+            d_cols = slice(hs[0] * HALF, (hs[-1] + 1) * HALF)
+            nc.sync.dma_start(out=y_rows[j * P : (j + 1) * P, d_cols], in_=y[j][:, d_cols])
+
+        def Sc(js, hs=(0, 1)):
+            cols = slice(js[0] * P, (js[-1] + 1) * P)
+            h_sl = slice(hs[0], hs[-1] + 1)
+            nc.sync.dma_start(out=codes_hbm[:, h_sl, cols], in_=y_codes[:, h_sl, cols].bitcast(I32))
+
+        def Ss(j0, j1):
+            cols = slice(j0 * P, j1 * P)
+            for q in range(4):
+                nc.sync.dma_start(
+                    out=scales_hbm[4 * q : 4 * q + 4, :, cols].bitcast(I32),
+                    in_=y_plane[32 * q : 32 * q + 4, :, cols].bitcast(I32),
+                )
+
+        def setup():
+            nc.scalar.dma_start(out=base_rows[:, :, 0:8], in_=default_vec.rearrange("e (k w) -> k e w", w=8))
+            nc.vector.memset(logit_rows[:], 0.0)
+            nc.vector.memset(x_plane[:].bitcast(I32), 0)
+            nc.vector.memset(warm[:], 0.0)
+            make_identity(nc, ident[:])
+            nc.scalar.dma_start(
+                out=logit_rows[0:TILES, :], in_=capacity_logit.rearrange("e c -> (e c)").rearrange("(j p) -> j p", p=P)
+            )
+            for q in range(4):
+                nc.scalar.dma_start(
+                    out=x_plane[32 * q : 32 * q + 16, :].bitcast(I32), in_=x_scales[:, 4 * q : 4 * q + 4, :].bitcast(I32)
+                )
+            nc.scalar.activation(out=warm_out[:], in_=warm[:], func=ACT.Sigmoid)
+            nc.vector.tensor_copy(out=ident_bf[:], in_=ident[:])
+
+        def TL(b):
+            turned["logit"] = bank(b, BF16, P)
+            nc.tensor.transpose(turned["logit"][:], logit_rows[:], ident_bf[:])
+
+        def SIG():
+            nc.scalar.activation(out=rest[:, 0:TILES], in_=turned["logit"][:, 0:TILES], func=ACT.Sigmoid, scale=-1.0)
+            nc.scalar.activation(out=mask[:, 0:TILES], in_=turned["logit"][:, 0:TILES], func=ACT.Sigmoid)
+
+        setup()
+        for g in range(3):
+            load_sel(0, g)
+            load_x(g)
+        load_sel(0, 3)
+        for g in range(2):
+            load_sel(1, g)
+        load_x(3)
+        for g in range(2, 4):
+            load_sel(1, g)
+        for c in (2, 3):
+            for g in range(4):
+                load_sel(c, g)
+        BE(0, 6); TL(3); BE(1, 7)
+        I0(0, "V"); Q0(0)
+        SIG()
+        BD(0, "a", "S"); BD(1, "a", "S"); BD(1, "b", "S"); BD(2, "a", "S")
+        for j in range(3):
+            MM0(0, j)
+        BE(2, 6)
+        I0(1, "V"); Q0(1)
+        for j in range(3):
+            MM0(1, j)
+        BE(3, 7)
+        I0(2, "V"); Q0(2)
+        BD(3, "a", "S"); BD(4, "a", "S")
+        for j in range(3):
+            MM0(2, j)
+        I0(3, "V"); Q0(3)
+        BD(4, "b", "V"); BD(5, "a", "S")
+        I(3, "V", [0, 1]); I(4, "S", [0, 1]); I(3, "V", [2, 3]); Q(3)
+        for j in range(3):
+            MM0(3, j)
+        I(4, "S", [2, 3])
+        E(0, 0); E(0, 1); E(1, 0); E(1, 1); Q(4)
+        C(0, [0, 1], "S")
+        C(1, [0, 1], "V"); E(2, 0); E(2, 1)
+        Sy(0, [0, 1]); Sy(1, [0, 1]); Sy(2, [0, 1])
+        Tafter = {3: [0, 1], 5: [2, 3], 7: [4, 5], 9: [6, 7], 10: [8], 11: [9]}
+        Eafter = {3: [(4, 4)], 4: [(5, 5)], 6: [(6, 4)], 7: [(7, 5)]}
+        Bsteps = {4: [(6, "a")], 5: [(7, "a"), (7, "b")], 6: [(8, "a")], 7: [(9, "a")], 8: [(10, "a"), (10, "b")], 9: [(11, "a")]}
+        Xq = []
+        for j in range(3, 12):
+            MM(j, 0); MM(j, 1)
+            if j > 3:
+                E(j - 1, 1); Sy(j - 1, [0, 1])
+            if 4 < j + 1 < 12:
+                Q(j + 1)
+            C(j - 1, [0, 1], "V")
+            for t in Xq:
+                X(t, [0, 1], "S")
+            Zn = list(Xq)
+            Xq = []
+            if 4 < j + 2 < 12:
+                n = {3: 4, 4: 3, 5: 2, 6: 3, 7: 3, 8: 2, 9: 3}[j]
+                I(j + 2, "S", list(range(n)))
+                if n < 4:
+                    I(j + 2, "V", list(range(n, 4)))
+            for b in Bsteps.get(j, []):
+                BD(b[0], b[1], "S")
+            E(j, 0)
+            if Zn:
+                Z(Zn, 0); Z(Zn, 1); Sc(Zn)
+            for t in Tafter.get(j, []):
+                T(t, [0, 1])
+                Xq.append(t)
+            for e in Eafter.get(j, []):
+                BE(*e)
+        E(11, 1)
+        X(9, [0, 1], "S")
+        C(11, [0], "S"); Sy(11, [0, 1])
+        T(10, [0, 1]); C(11, [1], "V")
+        X(10, [0, 1], "S"); Z([9], 0); Z([9], 1); Sc([9]); Ss(0, 10); T(11, [0, 1]); Z([10], 0); Z([10], 1); Sc([10])
+        X(11, [0, 1], "S"); Z([11], 0); Z([11], 1); Sc([11]); Ss(10, 12)

@@ -21,8 +21,9 @@ PACK = 4
 PASSES = TOK // (P * PACK)
 HALF = 512
 TILES = SLOTS // P
-CHUNKS = [[0, 1, 2], [3, 4], [5, 6, 7], [8, 9, 10, 11]]
-GROUPS = [(0, 1), (2, 3), (4, 5), (6, 7), (8,), (9,), (10,), (11,)]
+CHUNKS = [[0, 1, 2, 3], [4, 5], [6, 7], [8, 9, 10, 11]]
+GROUPS = [(0, 1), (2, 3), (4, 5), (6, 7), (8, 9), (10,), (11,)]
+BASE_BANK = {0: 3, 1: 4, 2: 5, 3: 6, 4: 7, 5: 6, 6: 7, 7: 6, 8: 7, 9: 4, 10: 5, 11: 4}
 
 
 def tile_soft_capacity_dispatch_g6_kernel(
@@ -47,8 +48,9 @@ def tile_soft_capacity_dispatch_g6_kernel(
         ident_bf = keep.tile([P, P], BF16)
         warm = keep.tile([P, 8], F32)
         warm_out = keep.tile([P, 8], F32)
-        logit_rows = keep.tile([P, P], BF16)
-        base_rows = keep.tile([P, EXP, 16], BF16)
+        rows = keep.tile([P, D + P], BF16)
+        base_words = keep.tile([P, 4, EXP], F32)
+        mixed_words = keep.tile([P, EXP // 2, 4, P], F32)
         mask = keep.tile([P, 16], F32)
         rest = keep.tile([P, 16], F32)
         x_codes = keep.tile([P, PASSES, D], U32, align_bytes=64)
@@ -82,18 +84,20 @@ def tile_soft_capacity_dispatch_g6_kernel(
             rows = sel_rows[g * P * PACK : (g + 1) * P * PACK, js[0] * P : (js[-1] + 1) * P]
             nc.sync.dma_start(out=raw[c][:, g], in_=rows.rearrange("(p t) w -> p t w", t=PACK))
 
-        def load_x(g):
-            nc.sync.dma_start(out=x_codes[:, g, :].bitcast(I32), in_=x_words[g].rearrange("p n t -> p (n t)").bitcast(I32))
+        def load_x(g, hs):
+            d_cols = slice(hs[0] * HALF, (hs[-1] + 1) * HALF)
+            words = x_words[g].rearrange("p n t -> p (n t)").bitcast(I32)
+            nc.sync.dma_start(out=x_codes[:, g, d_cols].bitcast(I32), in_=words[:, d_cols])
 
         def I0(g, name):
             width = P * len(first)
-            staged["first", g] = ring.tile([P, PASSES * P * PACK], BF16, name="staged", tag="staged", align_bytes=64)
+            staged["first", g] = ring.tile([P, PASSES * P * PACK], BF16, name="staged", tag="staged", bufs=4, align_bytes=64)
             dst = staged["first", g][:, : width * PACK].rearrange("p (c i t) -> p c t i", i=4, t=PACK)
             copy(name, dst, raw[0][:, g].rearrange("p t (c i) -> p c t i", i=4))
 
         def Q0(g):
             width = P * len(first)
-            for lo, hi in ((0, 256), (256, width)):
+            for lo, hi in ((0, width),):
                 cols = slice(g * width + lo, g * width + hi)
                 nc.vector.quantize_mx(
                     out=sel_codes[:, cols].bitcast(FP8X4),
@@ -103,7 +107,7 @@ def tile_soft_capacity_dispatch_g6_kernel(
 
         def I(j, name, gs):
             if j not in staged:
-                staged[j] = ring.tile([P, PASSES * P * PACK], BF16, name="staged", tag="staged", align_bytes=64)
+                staged[j] = ring.tile([P, PASSES * P * PACK], BF16, name="staged", tag="staged", bufs=4, align_bytes=64)
             c = chunk_of[j]
             off = (j - CHUNKS[c][0]) * P
             g0, g1 = gs[0], gs[-1] + 1
@@ -117,7 +121,7 @@ def tile_soft_capacity_dispatch_g6_kernel(
 
         def mm(j, h, g):
             if g == 0:
-                sums[j, h] = bank(2 * j + h if j in first else 2 * ((j + 1) % 2) + h)
+                sums[j, h] = bank(2 * j + h if j < 3 else 2 * ((j + 1) % 2) + h)
             d_cols = slice(h * HALF, (h + 1) * HALF)
             nc.tensor.matmul_mx(
                 out=sums[j, h][:],
@@ -137,24 +141,38 @@ def tile_soft_capacity_dispatch_g6_kernel(
             for g in range(PASSES):
                 mm(j, h, g)
 
-        def BE(e, b):
-            base_bank[e] = bank(b)
-            words = base_rows[:].bitcast(F32)
-            for w in range(4):
-                nc.tensor.transpose(
-                    base_bank[e][:, w * P : (w + 1) * P], words[:, e, w : w + 1].to_broadcast([P, P]), ident[:]
-                )
+        def TR():
+            turned["base"] = bank(1)
+            words = rows[:, :D].bitcast(F32)
+            for c in range(4):
+                nc.tensor.transpose(turned["base"][:, c * P : (c + 1) * P], words[:, c * P : (c + 1) * P], ident[:])
 
-        def BD(j, part, name):
-            mixed = j % 3 == 1
-            e = 2 * (j // 3) + (0 if j % 3 == 0 or (mixed and part == "a") else 1)
-            rows = slice(0, P) if not mixed else (slice(0, 64) if part == "a" else slice(64, P))
-            src = base_bank[e][rows, :].bitcast(BF16).rearrange("p (w n b) -> p n w b", w=4, b=2)
-            dst = y[j][rows, :].rearrange("p (n w b) -> p n w b", w=4, b=2)
+        def XR(name):
+            copy(name, base_words[:], turned["base"][:].rearrange("p (c e) -> p c e", c=4)[:, :, :EXP])
+
+        def MAT(q0, q1):
+            words = base_words[:].rearrange("p c (q s) -> p q c s", s=2)[:, q0:q1]
+            nc.vector.tensor_copy(
+                out=mixed_words[:, q0:q1].rearrange("p q c (s r) -> p q c s r", s=2),
+                in_=words.unsqueeze(4).to_broadcast([P, q1 - q0, 4, 2, 64]),
+            )
+
+        def BE(j):
+            base_bank[j] = bank(BASE_BANK[j])
+            for c in range(4):
+                if j % 3 == 1:
+                    columns = mixed_words[:, j // 3, c, :]
+                else:
+                    e = 2 * (j // 3) + j % 3 // 2
+                    columns = base_words[:, c, e : e + 1].to_broadcast([P, P])
+                nc.tensor.transpose(base_bank[j][:, c * P : (c + 1) * P], columns, ident[:])
+
+        def B(j, name):
+            src = base_bank[j][:].bitcast(BF16)
             if name == "V":
-                nc.vector.tensor_scalar(out=dst, in0=src, scalar1=rest[rows, j : j + 1], scalar2=None, op0=ALU.mult)
+                nc.vector.tensor_scalar(out=y[j][:], in0=src, scalar1=rest[:, j : j + 1], scalar2=None, op0=ALU.mult)
             else:
-                nc.scalar.activation(out=dst, in_=src, func=ACT.Copy, scale=rest[rows, j : j + 1])
+                nc.scalar.activation(out=y[j][:], in_=src, func=ACT.Copy, scale=rest[:, j : j + 1])
 
         def E(j, h):
             part = y[j][:, h * HALF : (h + 1) * HALF]
@@ -171,13 +189,12 @@ def tile_soft_capacity_dispatch_g6_kernel(
             copy(name, dst, src)
 
         def T(j, hs):
-            if j not in turned:
-                turned[j] = bank(6 + j % 2)
+            turned[j, hs] = bank(6 + j % 2 if j < 11 else 4 + hs[0])
             words = y_pairs[j][:].bitcast(F32)
             for h in hs:
                 for u in range(2):
                     cols = slice((2 * h + u) * P, (2 * h + u + 1) * P)
-                    nc.tensor.transpose(turned[j][:, cols], words[:, cols], ident[:])
+                    nc.tensor.transpose(turned[j, hs][:, cols], words[:, cols], ident[:])
 
         def X(j, hs, name):
             js = group_of[j]
@@ -186,7 +203,7 @@ def tile_soft_capacity_dispatch_g6_kernel(
             off = (j - js[0]) * P
             h0, h1 = hs[0], hs[-1] + 1
             dst = y_turned[js][:].bitcast(F32).rearrange("p h (r u) -> p h r u", u=2)[:, h0:h1, off : off + P, :]
-            src = turned[j][:].rearrange("p (h u r) -> p h r u", h=2, u=2)[:, h0:h1]
+            src = turned[j, hs][:].rearrange("p (h u r) -> p h r u", h=2, u=2)[:, h0:h1]
             copy(name, dst, src)
 
         def Z(js, h):
@@ -210,22 +227,24 @@ def tile_soft_capacity_dispatch_g6_kernel(
         def Ss(j0, j1):
             cols = slice(j0 * P, j1 * P)
             for q in range(4):
-                nc.sync.dma_start(
+                (nc.sync if j0 == 0 else nc.scalar).dma_start(
                     out=scales_hbm[4 * q : 4 * q + 4, :, cols].bitcast(I32),
                     in_=y_plane[32 * q : 32 * q + 4, :, cols].bitcast(I32),
                 )
 
         def setup():
-            nc.scalar.dma_start(out=base_rows[:, :, 0:8], in_=default_vec.rearrange("e (k w) -> k e w", w=8))
-            nc.vector.memset(logit_rows[:], 0.0)
+            nc.scalar.dma_start(out=rows[0:32, :D], in_=default_vec.unsqueeze(0).to_broadcast([4, EXP, D]))
+            nc.vector.memset(rows[:, D:].bitcast(I32), 0)
             nc.vector.memset(x_plane[:].bitcast(I32), 0)
             nc.vector.memset(warm[:], 0.0)
+            nc.vector.memset(rows[32:64, :D].bitcast(I32), 0)
+            nc.vector.memset(rows[64:P, :D].bitcast(I32), 0)
             make_identity(nc, ident[:])
             nc.scalar.dma_start(
-                out=logit_rows[0:TILES, :], in_=capacity_logit.rearrange("e c -> (e c)").rearrange("(j p) -> j p", p=P)
+                out=rows[0:TILES, D:], in_=capacity_logit.rearrange("e c -> (e c)").rearrange("(j p) -> j p", p=P)
             )
             for q in range(4):
-                nc.scalar.dma_start(
+                (nc.scalar if q < 2 else nc.gpsimd).dma_start(
                     out=x_plane[32 * q : 32 * q + 16, :].bitcast(I32), in_=x_scales[:, 4 * q : 4 * q + 4, :].bitcast(I32)
                 )
             nc.scalar.activation(out=warm_out[:], in_=warm[:], func=ACT.Sigmoid)
@@ -233,83 +252,239 @@ def tile_soft_capacity_dispatch_g6_kernel(
 
         def TL(b):
             turned["logit"] = bank(b, BF16, P)
-            nc.tensor.transpose(turned["logit"][:], logit_rows[:], ident_bf[:])
+            nc.tensor.transpose(turned["logit"][:], rows[:, D:], ident_bf[:])
 
         def SIG():
             nc.scalar.activation(out=rest[:, 0:TILES], in_=turned["logit"][:, 0:TILES], func=ACT.Sigmoid, scale=-1.0)
             nc.scalar.activation(out=mask[:, 0:TILES], in_=turned["logit"][:, 0:TILES], func=ACT.Sigmoid)
 
         setup()
-        for g in range(3):
-            load_sel(0, g)
-            load_x(g)
-        load_sel(0, 3)
-        for g in range(2):
-            load_sel(1, g)
-        load_x(3)
-        for g in range(2, 4):
-            load_sel(1, g)
-        for c in (2, 3):
-            for g in range(4):
-                load_sel(c, g)
-        BE(0, 6); TL(3); BE(1, 7)
-        I0(0, "V"); Q0(0)
+        load_sel(0, 0)
+        TR()
+        XR("S")
+        I0(0, "V")
+        MAT(0, 1)
+        load_x(0, (1,))
+        load_sel(0, 1)
+        Q0(0)
+        MAT(1, 4)
+        TL(2)
+        BE(0)
+        BE(1)
+        load_x(0, (0,))
+        BE(2)
+        load_x(1, (1,))
+        BE(3)
         SIG()
-        BD(0, "a", "S"); BD(1, "a", "S"); BD(1, "b", "S"); BD(2, "a", "S")
-        for j in range(3):
-            MM0(0, j)
-        BE(2, 6)
-        I0(1, "V"); Q0(1)
-        for j in range(3):
-            MM0(1, j)
-        BE(3, 7)
-        I0(2, "V"); Q0(2)
-        BD(3, "a", "S"); BD(4, "a", "S")
-        for j in range(3):
-            MM0(2, j)
-        I0(3, "V"); Q0(3)
-        BD(4, "b", "V"); BD(5, "a", "S")
-        I(3, "V", [0, 1]); I(4, "S", [0, 1]); I(3, "V", [2, 3]); Q(3)
-        for j in range(3):
-            MM0(3, j)
-        I(4, "S", [2, 3])
-        E(0, 0); E(0, 1); E(1, 0); E(1, 1); Q(4)
-        C(0, [0, 1], "S")
-        C(1, [0, 1], "V"); E(2, 0); E(2, 1)
-        Sy(0, [0, 1]); Sy(1, [0, 1]); Sy(2, [0, 1])
-        Tafter = {3: [0, 1], 5: [2, 3], 7: [4, 5], 9: [6, 7], 10: [8], 11: [9]}
-        Eafter = {3: [(4, 4)], 4: [(5, 5)], 6: [(6, 4)], 7: [(7, 5)]}
-        Bsteps = {4: [(6, "a")], 5: [(7, "a"), (7, "b")], 6: [(8, "a")], 7: [(9, "a")], 8: [(10, "a"), (10, "b")], 9: [(11, "a")]}
-        Xq = []
-        for j in range(3, 12):
-            MM(j, 0); MM(j, 1)
-            if j > 3:
-                E(j - 1, 1); Sy(j - 1, [0, 1])
-            if 4 < j + 1 < 12:
-                Q(j + 1)
-            C(j - 1, [0, 1], "V")
-            for t in Xq:
-                X(t, [0, 1], "S")
-            Zn = list(Xq)
-            Xq = []
-            if 4 < j + 2 < 12:
-                n = {3: 4, 4: 3, 5: 2, 6: 3, 7: 3, 8: 2, 9: 3}[j]
-                I(j + 2, "S", list(range(n)))
-                if n < 4:
-                    I(j + 2, "V", list(range(n, 4)))
-            for b in Bsteps.get(j, []):
-                BD(b[0], b[1], "S")
-            E(j, 0)
-            if Zn:
-                Z(Zn, 0); Z(Zn, 1); Sc(Zn)
-            for t in Tafter.get(j, []):
-                T(t, [0, 1])
-                Xq.append(t)
-            for e in Eafter.get(j, []):
-                BE(*e)
+        mm(0, 0, 0)
+        load_sel(0, 2)
+        load_x(1, (0,))
+        load_sel(0, 3)
+        B(0, "S")
+        load_sel(1, 0)
+        I0(1, "V")
+        BE(4)
+        load_sel(1, 1)
+        mm(1, 0, 0)
+        B(1, "S")
+        mm(0, 1, 0)
+        B(2, "S")
+        I0(2, "V")
+        Q0(1)
+        B(3, "S")
+        I0(3, "V")
+        load_sel(1, 2)
+        mm(2, 0, 0)
+        mm(1, 1, 0)
+        load_sel(1, 3)
+        B(4, "S")
+        BE(5)
+        mm(2, 1, 0)
+        BE(6)
+        B(5, "S")
+        load_x(2, (0,))
+        Q0(2)
+        mm(2, 0, 1)
+        load_x(3, (0,))
+        mm(1, 0, 1)
+        Q0(3)
+        BE(7)
+        mm(0, 0, 1)
+        mm(1, 1, 1)
+        mm(0, 0, 2)
+        I(4, "V", [0, 1, 2, 3])
+        B(6, "S")
+        load_x(2, (1,))
+        mm(2, 0, 2)
+        B(7, "S")
+        I(5, "S", [0, 1, 2, 3])
+        mm(2, 0, 3)
+        mm(1, 0, 2)
+        E(2, 0)
+        load_x(3, (1,))
+        load_sel(2, 0)
+        mm(0, 0, 3)
+        mm(0, 1, 1)
+        mm(0, 1, 2)
+        E(0, 0)
+        mm(0, 1, 3)
+        BE(8)
+        mm(3, 0, 0)
+        B(8, "S")
+        mm(1, 0, 3)
+        load_sel(2, 1)
+        load_sel(2, 2)
+        mm(1, 1, 2)
+        mm(1, 1, 3)
+        mm(2, 1, 1)
+        Q(4)
+        E(0, 1)
+        Q(5)
+        mm(3, 0, 1)
+        I(6, "S", [0, 1, 2])
+        mm(2, 1, 2)
+        I(7, "S", [0, 1])
+        E(1, 0)
+        load_sel(2, 3)
+        load_sel(3, 0)
+        load_sel(3, 1)
+        mm(2, 1, 3)
+        mm(3, 0, 2)
+        mm(3, 1, 0)
+        load_sel(3, 2)
+        E(1, 1)
+        mm(3, 1, 1)
+        C(0, (0, 1), "S")
+        I(6, "V", [3])
+        C(1, (0, 1), "V")
+        E(2, 1)
+        Q(6)
+        mm(3, 0, 3)
+        MM(4, 0)
+        load_sel(3, 3)
+        Sy(0, (0, 1))
+        Sy(1, (0, 1))
+        Sy(2, (0, 1))
+        I(7, "V", [2, 3])
+        I(8, "S", [0, 1, 2])
+        mm(3, 1, 2)
+        mm(3, 1, 3)
+        E(3, 0)
+        I(9, "S", [0, 1])
+        E(3, 1)
+        Sy(3, (0, 1))
+        Q(7)
+        MM(4, 1)
+        BE(9)
+        I(8, "V", [3])
+        C(2, (0, 1), "S")
+        T(0, (0, 1))
+        BE(10)
+        E(4, 0)
+        T(1, (0, 1))
+        E(4, 1)
+        Sy(4, (0, 1))
+        MM(5, 0)
+        C(3, (0, 1), "V")
+        MM(5, 1)
+        MM(6, 0)
+        E(5, 0)
+        E(5, 1)
+        Sy(5, (0, 1))
+        I(9, "V", [2, 3])
+        X(0, (0, 1), "S")
+        T(2, (0, 1))
+        X(1, (0, 1), "S")
+        Z((0, 1), 0)
+        B(9, "S")
+        X(2, (0, 1), "S")
+        B(10, "S")
+        Q(8)
+        T(3, (0, 1))
+        X(3, (0, 1), "S")
+        C(4, (0, 1), "V")
+        MM(6, 1)
+        E(6, 0)
+        E(6, 1)
+        Sy(6, (0, 1))
+        MM(7, 0)
+        MM(7, 1)
+        Z((0, 1), 1)
+        Sc((0, 1), (0, 1))
+        C(5, (0, 1), "V")
+        Q(9)
+        T(4, (0, 1))
+        E(7, 0)
+        C(6, (0, 1), "S")
+        I(10, "S", [0, 1, 2, 3])
+        MM(8, 0)
+        E(7, 1)
+        Sy(7, (0, 1))
+        T(5, (0, 1))
+        MM(8, 1)
+        X(4, (0, 1), "V")
+        Z((2, 3), 0)
+        X(5, (0, 1), "S")
+        MM(9, 0)
+        MM(9, 1)
+        E(8, 0)
+        C(7, (0, 1), "V")
+        T(6, (0, 1))
+        E(8, 1)
+        Sy(8, (0, 1))
+        Z((2, 3), 1)
+        Sc((2, 3), (0, 1))
+        I(11, "S", [0, 1, 2, 3])
+        Q(10)
+        T(7, (0, 1))
+        X(6, (0, 1), "S")
+        BE(11)
+        E(9, 0)
+        Z((4, 5), 0)
+        E(9, 1)
+        Sy(9, (0, 1))
+        Z((4, 5), 1)
+        Sc((4, 5), (0, 1))
+        X(7, (0, 1), "S")
+        MM(10, 0)
+        C(8, (0, 1), "S")
+        MM(10, 1)
+        C(9, (0, 1), "V")
+        E(10, 0)
+        B(11, "S")
+        T(8, (0, 1))
+        Q(11)
+        T(9, (0, 1))
+        E(10, 1)
+        Sy(10, (0, 1))
+        X(8, (0, 1), "S")
+        Z((6, 7), 0)
+        Z((6, 7), 1)
+        Sc((6, 7), (0, 1))
+        MM(11, 0)
+        X(9, (0, 1), "S")
+        MM(11, 1)
+        Z((8, 9), 0)
+        Z((8, 9), 1)
+        Sc((8, 9), (0, 1))
+        Ss(0, 10)
+        C(10, (0, 1), "S")
+        E(11, 0)
+        Sy(11, (0,))
         E(11, 1)
-        X(9, [0, 1], "S")
-        C(11, [0], "S"); Sy(11, [0, 1])
-        T(10, [0, 1]); C(11, [1], "V")
-        X(10, [0, 1], "S"); Z([9], 0); Z([9], 1); Sc([9]); Ss(0, 10); T(11, [0, 1]); Z([10], 0); Z([10], 1); Sc([10])
-        X(11, [0, 1], "S"); Z([11], 0); Z([11], 1); Sc([11]); Ss(10, 12)
+        Sy(11, (1,))
+        C(11, (0,), "S")
+        C(11, (1,), "V")
+        T(10, (0, 1))
+        X(10, (0, 1), "S")
+        T(11, (0,))
+        Z((10,), 0)
+        Z((10,), 1)
+        Sc((10,), (0, 1))
+        T(11, (1,))
+        X(11, (0,), "S")
+        Z((11,), 0)
+        X(11, (1,), "S")
+        Z((11,), 1)
+        Sc((11,), (0, 1))
+        Ss(10, 12)

@@ -24,6 +24,7 @@ TILES = SLOTS // P
 CHUNKS = [[0, 1, 2, 3], [4, 5], [6, 7], [8, 9, 10, 11]]
 GROUPS = [(0, 1), (2, 3), (4, 5), (6, 7), (8, 9), (10,), (11,)]
 BASE_BANK = {0: 3, 1: 4, 2: 5, 3: 6, 4: 7, 5: 6, 6: 7, 7: 6, 8: 7, 9: 4, 10: 5, 11: 4}
+POOL_COLS = 40
 
 
 def tile_soft_capacity_dispatch_g6_kernel(
@@ -91,7 +92,7 @@ def tile_soft_capacity_dispatch_g6_kernel(
 
         def I0(g, name):
             width = P * len(first)
-            staged["first", g] = ring.tile([P, PASSES * P * PACK], BF16, name="staged", tag="staged", bufs=4, align_bytes=64)
+            staged["first", g] = ring.tile([P, PASSES * P * PACK], BF16, name="staged_first", tag="staged_first", align_bytes=64)
             dst = staged["first", g][:, : width * PACK].rearrange("p (c i t) -> p c t i", i=4, t=PACK)
             copy(name, dst, raw[0][:, g].rearrange("p t (c i) -> p c t i", i=4))
 
@@ -105,14 +106,26 @@ def tile_soft_capacity_dispatch_g6_kernel(
                     in_=staged["first", g][:, lo * PACK : hi * PACK],
                 )
 
-        def I(j, name, gs):
+        def stage_tile(j):
             if j not in staged:
-                staged[j] = ring.tile([P, PASSES * P * PACK], BF16, name="staged", tag="staged", bufs=4, align_bytes=64)
+                tag = "staged%d" % (j % 2)
+                staged[j] = ring.tile([P, PASSES * P * PACK], BF16, name=tag, tag=tag, bufs=1, align_bytes=64)
+            return staged[j]
+
+        def G(j):
             c = chunk_of[j]
             off = (j - CHUNKS[c][0]) * P
+            dst = stage_tile(j)[:].rearrange("p (g w t) -> p g w t", g=PASSES, t=PACK)[:, :, :POOL_COLS, :]
+            src = raw[c][:, :, :, off : off + POOL_COLS].rearrange("p g t w -> p g w t")
+            nc.gpsimd.tensor_scalar(out=dst, in0=src, scalar1=1.0, scalar2=0.0, op0=ALU.mult, op1=ALU.add)
+
+        def I(j, name, gs):
+            c = chunk_of[j]
+            skip = POOL_COLS if j >= 6 else 0
+            off = (j - CHUNKS[c][0]) * P
             g0, g1 = gs[0], gs[-1] + 1
-            dst = staged[j][:].rearrange("p (g c i t) -> p g c t i", g=PASSES, i=4, t=PACK)[:, g0:g1]
-            src = raw[c][:, g0:g1, :, off : off + P].rearrange("p g t (c i) -> p g c t i", i=4)
+            dst = stage_tile(j)[:].rearrange("p (g c i t) -> p g c t i", g=PASSES, i=4, t=PACK)[:, g0:g1, skip // 4 :]
+            src = raw[c][:, g0:g1, :, off + skip : off + P].rearrange("p g t (c i) -> p g c t i", i=4)
             copy(name, dst, src)
 
         def Q(j):
@@ -259,230 +272,233 @@ def tile_soft_capacity_dispatch_g6_kernel(
             nc.scalar.activation(out=mask[:, 0:TILES], in_=turned["logit"][:, 0:TILES], func=ACT.Sigmoid)
 
         setup()
-        load_sel(0, 0)
         TR()
-        XR("S")
-        I0(0, "V")
-        MAT(0, 1)
+        load_sel(0, 0)
         load_x(0, (1,))
+        TL(2)
+        XR("S")
+        SIG()
+        load_x(1, (0,))
         load_sel(0, 1)
+        I0(0, "V")
+        load_x(1, (1,))
+        MAT(0, 1)
         Q0(0)
         MAT(1, 4)
-        TL(2)
         BE(0)
         BE(1)
+        mm(0, 1, 0)
+        load_sel(0, 2)
         load_x(0, (0,))
         BE(2)
-        load_x(1, (1,))
         BE(3)
-        SIG()
-        mm(0, 0, 0)
-        load_sel(0, 2)
-        load_x(1, (0,))
-        load_sel(0, 3)
-        B(0, "S")
-        load_sel(1, 0)
-        I0(1, "V")
-        BE(4)
-        load_sel(1, 1)
-        mm(1, 0, 0)
-        B(1, "S")
-        mm(0, 1, 0)
-        B(2, "S")
-        I0(2, "V")
-        Q0(1)
-        B(3, "S")
-        I0(3, "V")
-        load_sel(1, 2)
-        mm(2, 0, 0)
-        mm(1, 1, 0)
-        load_sel(1, 3)
-        B(4, "S")
-        BE(5)
-        mm(2, 1, 0)
-        BE(6)
-        B(5, "S")
         load_x(2, (0,))
-        Q0(2)
-        mm(2, 0, 1)
-        load_x(3, (0,))
-        mm(1, 0, 1)
-        Q0(3)
-        BE(7)
+        BE(4)
+        I0(1, "V")
+        B(0, "S")
+        mm(1, 1, 0)
+        Q0(1)
+        B(1, "S")
+        load_sel(0, 3)
+        load_sel(1, 0)
+        mm(0, 0, 0)
+        I0(2, "V")
+        mm(2, 0, 0)
+        load_sel(1, 1)
+        B(2, "S")
         mm(0, 0, 1)
+        Q0(2)
+        mm(1, 0, 0)
+        mm(2, 0, 1)
+        mm(1, 0, 1)
+        load_sel(1, 2)
+        B(3, "S")
+        BE(5)
+        I0(3, "V")
         mm(1, 1, 1)
+        mm(2, 1, 0)
+        load_sel(1, 3)
+        Q0(3)
         mm(0, 0, 2)
-        I(4, "V", [0, 1, 2, 3])
-        B(6, "S")
+        B(4, "S")
         load_x(2, (1,))
-        mm(2, 0, 2)
-        B(7, "S")
-        I(5, "S", [0, 1, 2, 3])
-        mm(2, 0, 3)
-        mm(1, 0, 2)
-        E(2, 0)
-        load_x(3, (1,))
-        load_sel(2, 0)
-        mm(0, 0, 3)
-        mm(0, 1, 1)
-        mm(0, 1, 2)
-        E(0, 0)
-        mm(0, 1, 3)
-        BE(8)
-        mm(3, 0, 0)
-        B(8, "S")
-        mm(1, 0, 3)
-        load_sel(2, 1)
-        load_sel(2, 2)
-        mm(1, 1, 2)
-        mm(1, 1, 3)
+        B(5, "S")
+        I(4, "V", [3])
+        I(4, "S", [0, 1, 2])
         mm(2, 1, 1)
-        Q(4)
+        load_x(3, (1,))
+        mm(0, 1, 1)
+        BE(6)
+        load_x(3, (0,))
+        BE(7)
+        B(6, "S")
+        mm(2, 0, 2)
+        load_sel(2, 0)
+        mm(0, 1, 2)
+        mm(1, 1, 2)
+        mm(0, 1, 3)
+        mm(1, 1, 3)
+        I(5, "V", [0, 1, 2, 3])
         E(0, 1)
-        Q(5)
-        mm(3, 0, 1)
-        I(6, "S", [0, 1, 2])
         mm(2, 1, 2)
-        I(7, "S", [0, 1])
-        E(1, 0)
-        load_sel(2, 3)
-        load_sel(3, 0)
-        load_sel(3, 1)
-        mm(2, 1, 3)
-        mm(3, 0, 2)
-        mm(3, 1, 0)
-        load_sel(3, 2)
+        mm(0, 0, 3)
         E(1, 1)
-        mm(3, 1, 1)
+        mm(1, 0, 2)
+        BE(8)
+        E(0, 0)
+        load_sel(2, 1)
+        B(7, "S")
+        mm(3, 1, 0)
+        load_sel(2, 2)
+        B(8, "S")
         C(0, (0, 1), "S")
-        I(6, "V", [3])
-        C(1, (0, 1), "V")
-        E(2, 1)
-        Q(6)
+        mm(1, 0, 3)
+        mm(2, 1, 3)
+        mm(3, 1, 1)
+        mm(2, 0, 3)
+        mm(3, 1, 2)
+        mm(3, 0, 0)
+        mm(3, 0, 1)
+        mm(3, 0, 2)
+        load_sel(2, 3)
+        Q(4)
+        G(6)
+        E(1, 0)
+        load_sel(3, 0)
         mm(3, 0, 3)
-        MM(4, 0)
+        E(2, 0)
+        C(1, (0, 1), "S")
+        mm(3, 1, 3)
+        load_sel(3, 1)
+        load_sel(3, 2)
+        Q(5)
+        G(7)
+        T(0, (0, 1))
+        BE(9)
         load_sel(3, 3)
         Sy(0, (0, 1))
         Sy(1, (0, 1))
+        E(2, 1)
         Sy(2, (0, 1))
-        I(7, "V", [2, 3])
-        I(8, "S", [0, 1, 2])
-        mm(3, 1, 2)
-        mm(3, 1, 3)
+        X(0, (0, 1), "S")
+        T(1, (0, 1))
         E(3, 0)
-        I(9, "S", [0, 1])
+        C(2, (0, 1), "S")
+        MM(4, 0)
+        X(1, (0, 1), "S")
+        MM(4, 1)
+        I(6, "V", [0, 1, 2, 3])
         E(3, 1)
         Sy(3, (0, 1))
-        Q(7)
-        MM(4, 1)
-        BE(9)
-        I(8, "V", [3])
-        C(2, (0, 1), "S")
-        T(0, (0, 1))
-        BE(10)
+        I(7, "V", [0, 1, 2, 3])
+        B(9, "S")
+        MM(5, 0)
+        Q(6)
+        G(8)
         E(4, 0)
-        T(1, (0, 1))
         E(4, 1)
         Sy(4, (0, 1))
-        MM(5, 0)
-        C(3, (0, 1), "V")
-        MM(5, 1)
-        MM(6, 0)
+        Q(7)
+        G(9)
         E(5, 0)
+        MM(5, 1)
         E(5, 1)
         Sy(5, (0, 1))
-        I(9, "V", [2, 3])
-        X(0, (0, 1), "S")
-        T(2, (0, 1))
-        X(1, (0, 1), "S")
         Z((0, 1), 0)
-        B(9, "S")
-        X(2, (0, 1), "S")
-        B(10, "S")
-        Q(8)
-        T(3, (0, 1))
-        X(3, (0, 1), "S")
-        C(4, (0, 1), "V")
-        MM(6, 1)
-        E(6, 0)
-        E(6, 1)
-        Sy(6, (0, 1))
-        MM(7, 0)
-        MM(7, 1)
+        MM(6, 0)
         Z((0, 1), 1)
         Sc((0, 1), (0, 1))
-        C(5, (0, 1), "V")
+        MM(6, 1)
+        C(3, (0, 1), "S")
+        I(8, "S", [0, 1, 2, 3])
+        T(2, (0, 1))
+        T(3, (0, 1))
+        Q(8)
+        G(10)
+        E(6, 0)
+        MM(7, 0)
+        I(9, "S", [0, 1, 2, 3])
+        E(6, 1)
+        Sy(6, (0, 1))
         Q(9)
-        T(4, (0, 1))
+        G(11)
+        X(2, (0, 1), "S")
+        C(4, (0, 1), "S")
         E(7, 0)
-        C(6, (0, 1), "S")
-        I(10, "S", [0, 1, 2, 3])
-        MM(8, 0)
+        X(3, (0, 1), "V")
+        C(5, (0, 1), "S")
+        MM(7, 1)
         E(7, 1)
         Sy(7, (0, 1))
-        T(5, (0, 1))
-        MM(8, 1)
-        X(4, (0, 1), "V")
-        Z((2, 3), 0)
-        X(5, (0, 1), "S")
-        MM(9, 0)
-        MM(9, 1)
+        MM(8, 0)
         E(8, 0)
-        C(7, (0, 1), "V")
-        T(6, (0, 1))
+        MM(8, 1)
+        I(10, "S", [0, 1, 2, 3])
+        Z((2, 3), 0)
         E(8, 1)
         Sy(8, (0, 1))
+        C(6, (0, 1), "V")
+        BE(10)
+        T(4, (0, 1))
+        T(5, (0, 1))
+        I(11, "S", [0, 1, 2, 3])
+        MM(9, 0)
+        X(4, (0, 1), "S")
+        Q(10)
+        X(5, (0, 1), "S")
+        C(7, (0, 1), "V")
+        MM(9, 1)
         Z((2, 3), 1)
         Sc((2, 3), (0, 1))
-        I(11, "S", [0, 1, 2, 3])
-        Q(10)
-        T(7, (0, 1))
-        X(6, (0, 1), "S")
-        BE(11)
+        T(6, (0, 1))
         E(9, 0)
-        Z((4, 5), 0)
+        B(10, "S")
+        T(7, (0, 1))
         E(9, 1)
         Sy(9, (0, 1))
+        Z((4, 5), 0)
+        Q(11)
+        MM(10, 0)
+        C(8, (0, 1), "V")
+        X(6, (0, 1), "S")
+        X(7, (0, 1), "S")
         Z((4, 5), 1)
         Sc((4, 5), (0, 1))
-        X(7, (0, 1), "S")
-        MM(10, 0)
-        C(8, (0, 1), "S")
         MM(10, 1)
-        C(9, (0, 1), "V")
         E(10, 0)
-        B(11, "S")
+        C(9, (0, 1), "S")
         T(8, (0, 1))
-        Q(11)
-        T(9, (0, 1))
         E(10, 1)
         Sy(10, (0, 1))
-        X(8, (0, 1), "S")
+        BE(11)
         Z((6, 7), 0)
+        X(8, (0, 1), "S")
+        B(11, "S")
+        T(9, (0, 1))
+        MM(11, 0)
+        C(10, (0, 1), "S")
+        X(9, (0, 1), "V")
+        MM(11, 1)
+        T(10, (0, 1))
         Z((6, 7), 1)
         Sc((6, 7), (0, 1))
-        MM(11, 0)
-        X(9, (0, 1), "S")
-        MM(11, 1)
         Z((8, 9), 0)
         Z((8, 9), 1)
         Sc((8, 9), (0, 1))
         Ss(0, 10)
-        C(10, (0, 1), "S")
         E(11, 0)
         Sy(11, (0,))
-        E(11, 1)
-        Sy(11, (1,))
         C(11, (0,), "S")
-        C(11, (1,), "V")
-        T(10, (0, 1))
         X(10, (0, 1), "S")
         T(11, (0,))
+        X(11, (0,), "S")
+        E(11, 1)
+        Sy(11, (1,))
+        C(11, (1,), "V")
         Z((10,), 0)
         Z((10,), 1)
         Sc((10,), (0, 1))
         T(11, (1,))
-        X(11, (0,), "S")
         Z((11,), 0)
         X(11, (1,), "S")
         Z((11,), 1)

from contextlib import ExitStack

import concourse.mybir as mybir
from concourse.masks import make_identity

TOK, EXP, CAP, D = 2048, 8, 192, 1024
SLOTS = EXP * CAP
FLOPS = 2 * TOK * SLOTS * D

F32 = mybir.dt.float32
BF16 = mybir.dt.bfloat16
I32 = mybir.dt.int32
U32 = mybir.dt.uint32
U8 = mybir.dt.uint8
FP8X4 = mybir.dt.float8_e4m3fn_x4
ACT = mybir.ActivationFunctionType
ALU = mybir.AluOpType

P = 128
PACK = 4
PASSES = TOK // (P * PACK)
HALF = 512
TILES = SLOTS // P
CHUNKS = [[0, 1, 2, 3], [4, 5], [6, 7], [8, 9, 10, 11]]
GROUPS = [(0, 1), (2, 3), (4, 5), (6, 7), (8, 9), (10,), (11,)]
BASE_BANK = {0: 3, 1: 4, 2: 5, 3: 6, 4: 7, 5: 6, 6: 7, 7: 6, 8: 7, 9: 4, 10: 5, 11: 4}
POOL_COLS = 40


def tile_soft_capacity_dispatch_g6_kernel(
    tc, x_words, x_scales, select, capacity_logit, default_vec, out_0, out_1, out_2
):
    nc = tc.nc
    sel_rows = select.rearrange("k e c -> k (e c)")
    y_rows = out_0.rearrange("e c d -> (e c) d")
    codes_hbm = out_1.rearrange("h p m t -> p h (m t)").bitcast(I32)
    scales_hbm = out_2.rearrange("h q m -> q h m")
    chunk_of = {j: c for c, js in enumerate(CHUNKS) for j in js}
    group_of = {j: js for js in GROUPS for j in js}
    first = CHUNKS[0]

    with ExitStack() as ctx:
        keep = ctx.enter_context(tc.tile_pool(name="keep", bufs=1))
        ring = ctx.enter_context(tc.tile_pool(name="ring", bufs=3))
        psum = ctx.enter_context(tc.psum_pool(name="psum", bufs=1))
        ctx.enter_context(tc.manual_schedule())

        ident = keep.tile([P, P], F32)
        ident_bf = keep.tile([P, P], BF16)
        warm = keep.tile([P, 8], F32)
        warm_out = keep.tile([P, 8], F32)
        rows = keep.tile([P, D + P], BF16)
        base_words = keep.tile([P, 4, EXP], F32)
        mixed_words = keep.tile([P, EXP // 2, 4, P], F32)
        mask = keep.tile([P, 16], F32)
        rest = keep.tile([P, 16], F32)
        x_codes = keep.tile([P, PASSES, D], U32, align_bytes=64)
        x_plane = keep.tile([P, D], U8, align_bytes=64)
        raw = [keep.tile([P, PASSES, PACK, P * len(js)], BF16, name="raw%d" % c) for c, js in enumerate(CHUNKS)]
        sel_codes = keep.tile([P, TILES * PASSES * P], U32, align_bytes=64)
        sel_plane = keep.tile([P, TILES * PASSES * P], U8, align_bytes=64)
        y = [keep.tile([P, D], F32, name="y%d" % j) for j in range(TILES)]
        y_codes = keep.tile([P, 2, SLOTS], U32, align_bytes=64)
        y_plane = keep.tile([P, 2, SLOTS], U8, align_bytes=64)
        staged, sums, base_bank, y_pairs, turned, y_turned = {}, {}, {}, {}, {}, {}

        def engine(name):
            return nc.vector if name == "V" else nc.scalar

        def copy(name, out, in_):
            if name == "V":
                nc.vector.tensor_copy(out=out, in_=in_)
            else:
                nc.scalar.copy(out=out, in_=in_)

        def bank(b, dtype=F32, width=HALF):
            return psum.tile([P, width], dtype, name="bank%d" % b, tag="bank%d" % b)

        def sel_cols(j, g):
            start = (g * len(first) + j) * P if j in first else (j * PASSES + g) * P
            return slice(start, start + P)

        def load_sel(c, g):
            js = CHUNKS[c]
            rows = sel_rows[g * P * PACK : (g + 1) * P * PACK, js[0] * P : (js[-1] + 1) * P]
            nc.sync.dma_start(out=raw[c][:, g], in_=rows.rearrange("(p t) w -> p t w", t=PACK))

        def load_x(g, hs):
            d_cols = slice(hs[0] * HALF, (hs[-1] + 1) * HALF)
            words = x_words[g].rearrange("p n t -> p (n t)").bitcast(I32)
            nc.sync.dma_start(out=x_codes[:, g, d_cols].bitcast(I32), in_=words[:, d_cols])

        def I0(g, name):
            width = P * len(first)
            staged["first", g] = ring.tile([P, PASSES * P * PACK], BF16, name="staged_first", tag="staged_first", align_bytes=64)
            dst = staged["first", g][:, : width * PACK].rearrange("p (c i t) -> p c t i", i=4, t=PACK)
            copy(name, dst, raw[0][:, g].rearrange("p t (c i) -> p c t i", i=4))

        def Q0(g):
            width = P * len(first)
            for lo, hi in ((0, width),):
                cols = slice(g * width + lo, g * width + hi)
                nc.vector.quantize_mx(
                    out=sel_codes[:, cols].bitcast(FP8X4),
                    scales=sel_plane[:, cols],
                    in_=staged["first", g][:, lo * PACK : hi * PACK],
                )

        def stage_tile(j):
            if j not in staged:
                tag = "staged%d" % (j % 2)
                staged[j] = ring.tile([P, PASSES * P * PACK], BF16, name=tag, tag=tag, bufs=1, align_bytes=64)
            return staged[j]

        def G(j):
            c = chunk_of[j]
            off = (j - CHUNKS[c][0]) * P
            dst = stage_tile(j)[:].rearrange("p (g w t) -> p g w t", g=PASSES, t=PACK)[:, :, :POOL_COLS, :]
            src = raw[c][:, :, :, off : off + POOL_COLS].rearrange("p g t w -> p g w t")
            nc.gpsimd.tensor_scalar(out=dst, in0=src, scalar1=1.0, scalar2=0.0, op0=ALU.mult, op1=ALU.add)

        def I(j, name, gs):
            c = chunk_of[j]
            skip = POOL_COLS if j >= 6 else 0
            off = (j - CHUNKS[c][0]) * P
            g0, g1 = gs[0], gs[-1] + 1
            dst = stage_tile(j)[:].rearrange("p (g c i t) -> p g c t i", g=PASSES, i=4, t=PACK)[:, g0:g1, skip // 4 :]
            src = raw[c][:, g0:g1, :, off + skip : off + P].rearrange("p g t (c i) -> p g c t i", i=4)
            copy(name, dst, src)

        def Q(j):
            cols = slice(j * PASSES * P, (j + 1) * PASSES * P)
            nc.vector.quantize_mx(out=sel_codes[:, cols].bitcast(FP8X4), scales=sel_plane[:, cols], in_=staged[j][:])

        def mm(j, h, g):
            if g == 0:
                sums[j, h] = bank(2 * j + h if j < 3 else 2 * ((j + 1) % 2) + h)
            d_cols = slice(h * HALF, (h + 1) * HALF)
            nc.tensor.matmul_mx(
                out=sums[j, h][:],
                lhsT=sel_codes[:, sel_cols(j, g)].bitcast(FP8X4),
                lhsT_scale=sel_plane[:, sel_cols(j, g)],
                rhs=x_codes[:, g, d_cols].bitcast(FP8X4),
                rhs_scale=x_plane[4 * g : P, d_cols],
                start=(g == 0),
                stop=(g == PASSES - 1),
            )

        def MM0(g, j):
            for h in range(2):
                mm(j, h, g)

        def MM(j, h):
            for g in range(PASSES):
                mm(j, h, g)

        def TR():
            turned["base"] = bank(1)
            words = rows[:, :D].bitcast(F32)
            for c in range(4):
                nc.tensor.transpose(turned["base"][:, c * P : (c + 1) * P], words[:, c * P : (c + 1) * P], ident[:])

        def XR(name):
            copy(name, base_words[:], turned["base"][:].rearrange("p (c e) -> p c e", c=4)[:, :, :EXP])

        def MAT(q0, q1):
            words = base_words[:].rearrange("p c (q s) -> p q c s", s=2)[:, q0:q1]
            nc.vector.tensor_copy(
                out=mixed_words[:, q0:q1].rearrange("p q c (s r) -> p q c s r", s=2),
                in_=words.unsqueeze(4).to_broadcast([P, q1 - q0, 4, 2, 64]),
            )

        def BE(j):
            base_bank[j] = bank(BASE_BANK[j])
            for c in range(4):
                if j % 3 == 1:
                    columns = mixed_words[:, j // 3, c, :]
                else:
                    e = 2 * (j // 3) + j % 3 // 2
                    columns = base_words[:, c, e : e + 1].to_broadcast([P, P])
                nc.tensor.transpose(base_bank[j][:, c * P : (c + 1) * P], columns, ident[:])

        def B(j, name):
            src = base_bank[j][:].bitcast(BF16)
            if name == "V":
                nc.vector.tensor_scalar(out=y[j][:], in0=src, scalar1=rest[:, j : j + 1], scalar2=None, op0=ALU.mult)
            else:
                nc.scalar.activation(out=y[j][:], in_=src, func=ACT.Copy, scale=rest[:, j : j + 1])

        def E(j, h):
            part = y[j][:, h * HALF : (h + 1) * HALF]
            nc.vector.scalar_tensor_tensor(
                out=part, in0=sums[j, h][:], scalar=mask[:, j : j + 1], in1=part, op0=ALU.mult, op1=ALU.add
            )

        def C(j, hs, name):
            if j not in y_pairs:
                y_pairs[j] = ring.tile([P, D], BF16, name="y_pairs", tag="y_pairs")
            h0, h1 = hs[0], hs[-1] + 1
            dst = y_pairs[j][:].rearrange("p (h u q e) -> p h u q e", h=2, u=2, e=2)[:, h0:h1]
            src = y[j][:].rearrange("p (h q u e) -> p h u q e", h=2, u=2, e=2)[:, h0:h1]
            copy(name, dst, src)

        def T(j, hs):
            turned[j, hs] = bank(6 + j % 2 if j < 11 else 4 + hs[0])
            words = y_pairs[j][:].bitcast(F32)
            for h in hs:
                for u in range(2):
                    cols = slice((2 * h + u) * P, (2 * h + u + 1) * P)
                    nc.tensor.transpose(turned[j, hs][:, cols], words[:, cols], ident[:])

        def X(j, hs, name):
            js = group_of[j]
            if js not in y_turned:
                y_turned[js] = ring.tile([P, 2, 2 * P * PACK], BF16, name="y_turned", tag="y_turned", align_bytes=64)
            off = (j - js[0]) * P
            h0, h1 = hs[0], hs[-1] + 1
            dst = y_turned[js][:].bitcast(F32).rearrange("p h (r u) -> p h r u", u=2)[:, h0:h1, off : off + P, :]
            src = turned[j, hs][:].rearrange("p (h u r) -> p h r u", h=2, u=2)[:, h0:h1]
            copy(name, dst, src)

        def Z(js, h):
            js = tuple(js)
            cols = slice(js[0] * P, (js[-1] + 1) * P)
            nc.vector.quantize_mx(
                out=y_codes[:, h, cols].bitcast(FP8X4),
                scales=y_plane[:, h, cols],
                in_=y_turned[js][:, h, : len(js) * P * PACK],
            )

        def Sy(j, hs):
            d_cols = slice(hs[0] * HALF, (hs[-1] + 1) * HALF)
            nc.sync.dma_start(out=y_rows[j * P : (j + 1) * P, d_cols], in_=y[j][:, d_cols])

        def Sc(js, hs=(0, 1)):
            cols = slice(js[0] * P, (js[-1] + 1) * P)
            h_sl = slice(hs[0], hs[-1] + 1)
            nc.sync.dma_start(out=codes_hbm[:, h_sl, cols], in_=y_codes[:, h_sl, cols].bitcast(I32))

        def Ss(j0, j1):
            cols = slice(j0 * P, j1 * P)
            for q in range(4):
                (nc.sync if j0 == 0 else nc.scalar).dma_start(
                    out=scales_hbm[4 * q : 4 * q + 4, :, cols].bitcast(I32),
                    in_=y_plane[32 * q : 32 * q + 4, :, cols].bitcast(I32),
                )

        def setup():
            nc.scalar.dma_start(out=rows[0:32, :D], in_=default_vec.unsqueeze(0).to_broadcast([4, EXP, D]))
            nc.vector.memset(rows[:, D:].bitcast(I32), 0)
            nc.vector.memset(x_plane[:].bitcast(I32), 0)
            nc.vector.memset(warm[:], 0.0)
            nc.vector.memset(rows[32:64, :D].bitcast(I32), 0)
            nc.vector.memset(rows[64:P, :D].bitcast(I32), 0)
            make_identity(nc, ident[:])
            nc.scalar.dma_start(
                out=rows[0:TILES, D:], in_=capacity_logit.rearrange("e c -> (e c)").rearrange("(j p) -> j p", p=P)
            )
            for q in range(4):
                (nc.scalar if q < 2 else nc.gpsimd).dma_start(
                    out=x_plane[32 * q : 32 * q + 16, :].bitcast(I32), in_=x_scales[:, 4 * q : 4 * q + 4, :].bitcast(I32)
                )
            nc.scalar.activation(out=warm_out[:], in_=warm[:], func=ACT.Sigmoid)
            nc.vector.tensor_copy(out=ident_bf[:], in_=ident[:])

        def TL(b):
            turned["logit"] = bank(b, BF16, P)
            nc.tensor.transpose(turned["logit"][:], rows[:, D:], ident_bf[:])

        def SIG():
            nc.scalar.activation(out=rest[:, 0:TILES], in_=turned["logit"][:, 0:TILES], func=ACT.Sigmoid, scale=-1.0)
            nc.scalar.activation(out=mask[:, 0:TILES], in_=turned["logit"][:, 0:TILES], func=ACT.Sigmoid)

        setup()
        TR()
        load_sel(0, 0)
        load_x(0, (1,))
        TL(2)
        XR("S")
        SIG()
        load_x(1, (0,))
        load_sel(0, 1)
        I0(0, "V")
        load_x(1, (1,))
        MAT(0, 1)
        Q0(0)
        MAT(1, 4)
        BE(0)
        BE(1)
        mm(0, 1, 0)
        load_sel(0, 2)
        load_x(0, (0,))
        BE(2)
        BE(3)
        load_x(2, (0,))
        BE(4)
        I0(1, "V")
        B(0, "S")
        mm(1, 1, 0)
        Q0(1)
        B(1, "S")
        load_sel(0, 3)
        load_sel(1, 0)
        mm(0, 0, 0)
        I0(2, "V")
        mm(2, 0, 0)
        load_sel(1, 1)
        B(2, "S")
        mm(0, 0, 1)
        Q0(2)
        mm(1, 0, 0)
        mm(2, 0, 1)
        mm(1, 0, 1)
        load_sel(1, 2)
        B(3, "S")
        BE(5)
        I0(3, "V")
        mm(1, 1, 1)
        mm(2, 1, 0)
        load_sel(1, 3)
        Q0(3)
        mm(0, 0, 2)
        B(4, "S")
        load_x(2, (1,))
        B(5, "S")
        I(4, "V", [3])
        I(4, "S", [0, 1, 2])
        mm(2, 1, 1)
        load_x(3, (1,))
        mm(0, 1, 1)
        BE(6)
        load_x(3, (0,))
        BE(7)
        B(6, "S")
        mm(2, 0, 2)
        load_sel(2, 0)
        mm(0, 1, 2)
        mm(1, 1, 2)
        mm(0, 1, 3)
        mm(1, 1, 3)
        I(5, "V", [0, 1, 2, 3])
        E(0, 1)
        mm(2, 1, 2)
        mm(0, 0, 3)
        E(1, 1)
        mm(1, 0, 2)
        BE(8)
        E(0, 0)
        load_sel(2, 1)
        B(7, "S")
        mm(3, 1, 0)
        load_sel(2, 2)
        B(8, "S")
        C(0, (0, 1), "S")
        mm(1, 0, 3)
        mm(2, 1, 3)
        mm(3, 1, 1)
        mm(2, 0, 3)
        mm(3, 1, 2)
        mm(3, 0, 0)
        mm(3, 0, 1)
        mm(3, 0, 2)
        load_sel(2, 3)
        Q(4)
        G(6)
        E(1, 0)
        load_sel(3, 0)
        mm(3, 0, 3)
        E(2, 0)
        C(1, (0, 1), "S")
        mm(3, 1, 3)
        load_sel(3, 1)
        load_sel(3, 2)
        Q(5)
        G(7)
        T(0, (0, 1))
        BE(9)
        load_sel(3, 3)
        Sy(0, (0, 1))
        Sy(1, (0, 1))
        E(2, 1)
        Sy(2, (0, 1))
        X(0, (0, 1), "S")
        T(1, (0, 1))
        E(3, 0)
        C(2, (0, 1), "S")
        MM(4, 0)
        X(1, (0, 1), "S")
        MM(4, 1)
        I(6, "V", [0, 1, 2, 3])
        E(3, 1)
        Sy(3, (0, 1))
        I(7, "V", [0, 1, 2, 3])
        B(9, "S")
        MM(5, 0)
        Q(6)
        G(8)
        E(4, 0)
        E(4, 1)
        Sy(4, (0, 1))
        Q(7)
        G(9)
        E(5, 0)
        MM(5, 1)
        E(5, 1)
        Sy(5, (0, 1))
        Z((0, 1), 0)
        MM(6, 0)
        Z((0, 1), 1)
        Sc((0, 1), (0, 1))
        MM(6, 1)
        C(3, (0, 1), "S")
        I(8, "S", [0, 1, 2, 3])
        T(2, (0, 1))
        T(3, (0, 1))
        Q(8)
        G(10)
        E(6, 0)
        MM(7, 0)
        I(9, "S", [0, 1, 2, 3])
        E(6, 1)
        Sy(6, (0, 1))
        Q(9)
        G(11)
        X(2, (0, 1), "S")
        C(4, (0, 1), "S")
        E(7, 0)
        X(3, (0, 1), "V")
        C(5, (0, 1), "S")
        MM(7, 1)
        E(7, 1)
        Sy(7, (0, 1))
        MM(8, 0)
        E(8, 0)
        MM(8, 1)
        I(10, "S", [0, 1, 2, 3])
        Z((2, 3), 0)
        E(8, 1)
        Sy(8, (0, 1))
        C(6, (0, 1), "V")
        BE(10)
        T(4, (0, 1))
        T(5, (0, 1))
        I(11, "S", [0, 1, 2, 3])
        MM(9, 0)
        X(4, (0, 1), "S")
        Q(10)
        X(5, (0, 1), "S")
        C(7, (0, 1), "V")
        MM(9, 1)
        Z((2, 3), 1)
        Sc((2, 3), (0, 1))
        T(6, (0, 1))
        E(9, 0)
        B(10, "S")
        T(7, (0, 1))
        E(9, 1)
        Sy(9, (0, 1))
        Z((4, 5), 0)
        Q(11)
        MM(10, 0)
        C(8, (0, 1), "V")
        X(6, (0, 1), "S")
        X(7, (0, 1), "S")
        Z((4, 5), 1)
        Sc((4, 5), (0, 1))
        MM(10, 1)
        E(10, 0)
        C(9, (0, 1), "S")
        T(8, (0, 1))
        E(10, 1)
        Sy(10, (0, 1))
        BE(11)
        Z((6, 7), 0)
        X(8, (0, 1), "S")
        B(11, "S")
        T(9, (0, 1))
        MM(11, 0)
        C(10, (0, 1), "S")
        X(9, (0, 1), "V")
        MM(11, 1)
        T(10, (0, 1))
        Z((6, 7), 1)
        Sc((6, 7), (0, 1))
        Z((8, 9), 0)
        Z((8, 9), 1)
        Sc((8, 9), (0, 1))
        Ss(0, 10)
        E(11, 0)
        Sy(11, (0,))
        C(11, (0,), "S")
        X(10, (0, 1), "S")
        T(11, (0,))
        X(11, (0,), "S")
        E(11, 1)
        Sy(11, (1,))
        C(11, (1,), "V")
        Z((10,), 0)
        Z((10,), 1)
        Sc((10,), (0, 1))
        T(11, (1,))
        Z((11,), 0)
        X(11, (1,), "S")
        Z((11,), 1)
        Sc((11,), (0, 1))
        Ss(10, 12)
